import numpy as np
import ml_dtypes


def mxq(x, axis, fmt="e4m3"):
    dtype, down = {"e4m3": (ml_dtypes.float8_e4m3fn, 7), "e5m2": (ml_dtypes.float8_e5m2, 14)}[fmt]
    v = np.moveaxis(np.asarray(x, np.float32).astype(ml_dtypes.bfloat16).astype(np.float64), axis, -1)
    blocks = v.reshape(v.shape[:-1] + (-1, 32))
    amax = np.abs(blocks).max(-1, keepdims=True)
    byte = np.maximum(np.where(amax > 0, np.frexp(amax)[1] - 1 + 127, 0) - down, 1)
    scale = np.exp2(byte - 127.0)
    codes = (blocks / scale).astype(np.float32).astype(dtype).astype(np.float64)
    return np.moveaxis((codes * scale).reshape(v.shape), -1, axis)


WIDE = False


def mx_kscale(k):
    if not WIDE:
        return np.ones(k)
    levels = np.array([10, -10, 5, -5, 0])
    if k % 512:
        return np.exp2(np.random.permutation(np.resize(levels, k // 32))).repeat(32)
    a = np.empty((k // 512, 16))
    for p in range(k // 512):
        a[p, :8] = np.random.permutation(np.resize(levels, 8))
        for g in range(8):
            far = levels[np.abs(levels - a[p, g]) >= 10]
            a[p, g + 8] = far[np.random.randint(len(far))]
    return np.exp2(a.ravel()).repeat(32)


def f64(x):
    return np.asarray(x).astype(np.float64)


def striped(idx):
    return np.tile(np.asarray(idx).reshape(-1, 16).T, (8, 1)).astype(np.uint16)


def unstriped(offs):
    return offs[:16].T.reshape(-1).astype(np.int64)


E2M1 = np.array([0.0, 0.5, 1.0, 1.5, 2.0, 3.0, 4.0, 6.0, -0.0, -0.5, -1.0, -1.5, -2.0, -3.0, -4.0, -6.0])


def pack_weight(w, fmt):
    k, n = w.shape
    w = f64(np.asarray(w, np.float32).astype(ml_dtypes.bfloat16)).reshape(k // 32, 32, n)
    amax = np.abs(w).max(1)
    if fmt == "e4m3":
        byte = np.frexp(amax)[1] - 1 + 127 - 7
    else:
        mant, ex = np.frexp(amax / 6.0)
        byte = np.where(mant > 0.5, ex, ex - 1) + 127
    byte = np.clip(np.where(amax > 0, byte, 1), 1, 254)
    scaled = (w * np.exp2(127.0 - byte)[:, None, :]).reshape(k, n).astype(np.float32)
    by_word = np.ascontiguousarray(scaled.reshape(k // 512, 128, 4, n).transpose(0, 1, 3, 2))
    if fmt == "e4m3":
        words = by_word.astype(ml_dtypes.float8_e4m3fn).view(np.uint8)
    else:
        c = by_word.astype(ml_dtypes.float4_e2m1fn).view(np.uint8) & 0xF
        words = (c[..., 0::2] | (c[..., 1::2] << 4)).reshape(k // 512, 128, 2 * n)
    return np.ascontiguousarray(words), np.ascontiguousarray(byte.astype(np.uint8).reshape(k // 512, 16, n))


def unpack_weight(words, scales, fmt):
    g, _, n = scales.shape
    words = np.ascontiguousarray(words).reshape(g, 128, n, -1)
    if fmt == "e4m3":
        vals = words.view(ml_dtypes.float8_e4m3fn).astype(np.float64)
    else:
        nib = np.empty((g, 128, n, 4), np.uint8)
        nib[..., 0::2] = words & 0xF
        nib[..., 1::2] = words >> 4
        vals = E2M1[nib]
    vals = vals * np.repeat(np.exp2(scales.astype(np.float64) - 127.0), 8, axis=1)[..., None]
    return vals.transpose(0, 1, 3, 2).reshape(g * 512, n)


K, R, F, T, J, M = 512, 128, 512, 2048, 512, 256


def setup_inputs():
    n = np.random.standard_normal
    idx = np.random.permutation(T)[:J]
    idx2 = np.random.permutation(J)[:M]
    idx3 = np.random.permutation(J)[:M]
    fk = mx_kscale(K)
    ff = mx_kscale(F)
    tabp = pack_weight(n((K, T)) / fk[:, None], "e4m3")
    return {
        "tab_words": tabp[0],
        "tab_scales": tabp[1],
        "w1": (n((K, R)) * 1 / np.sqrt(K) * fk[:, None]).astype(np.float32),
        "reserve": (np.random.uniform(0.3, 1.5, (R, 1))).astype(np.float32),
        "wo": (n((F, R)) * 1 / np.sqrt(F) * ff[:, None]).astype(np.float32),
        "dy": (n((F, M)) / ff[:, None]).astype(np.float32),
        "old": (0.5 * n((R, J))).astype(np.float32),
        "offs": striped(idx),
        "offs2": striped(idx2),
        "offs3": striped(idx3),
    }


def reference(tab_words, tab_scales, w1, reserve, wo, dy, old, offs, offs2, offs3):
    idx = unstriped(offs)
    idx2 = unstriped(offs2)
    idx3 = unstriped(offs3)
    tabu = unpack_weight(tab_words, tab_scales, "e4m3")
    w1q = mxq(f64(w1), 0, "e4m3")
    tabidxg = tabu[:, idx]
    a = w1q.T @ tabidxg
    h1 = np.exp(a)
    woq = mxq(f64(wo), 0, "e4m3")
    dyq = mxq(f64(dy), 0, "e4m3")
    c0 = woq.T @ dyq
    e1 = c0 / (h1[:, idx2] + h1[:, idx3] + f64(reserve))
    s1 = np.zeros((R, J))
    s1[:, idx2] = e1
    e2 = c0 * h1[:, idx2] / np.square(h1[:, idx2] + h1[:, idx3] + f64(reserve)) * (-1.0)
    s2 = np.zeros((R, J))
    s2[:, idx2] = e2
    e3 = c0 * h1[:, idx2] / np.square(h1[:, idx2] + h1[:, idx3] + f64(reserve)) * (-1.0)
    s3 = np.zeros((R, J))
    s3[:, idx3] = e3
    dh1 = s1 + s2 + s3
    da = dh1 * h1
    y = da + f64(old)
    return y

@@ -1,0 +1,146 @@
+from contextlib import ExitStack
+
+import concourse.mybir as mybir
+
+K, R, F, T, J, M = 512, 128, 512, 2048, 512, 256
+FLOPS = 2 * K * R * J + 2 * F * R * M
+
+F32 = mybir.dt.float32
+BF16 = mybir.dt.bfloat16
+I32 = mybir.dt.int32
+U32 = mybir.dt.uint32
+U16 = mybir.dt.uint16
+U8 = mybir.dt.uint8
+FP8X4 = mybir.dt.float8_e4m3fn_x4
+ACT = mybir.ActivationFunctionType
+ALU = mybir.AluOpType
+P = 128
+PACK = 4
+HALF = J // 2
+
+
+def tile_attend_cratiopairs_kernel(tc, tab_words, tab_scales, w1, reserve, wo, dy, old, offs, offs2, offs3, out):
+    nc = tc.nc
+    with ExitStack() as ctx:
+        keep = ctx.enter_context(tc.tile_pool(name="keep", bufs=1))
+        psum = ctx.enter_context(tc.psum_pool(name="psum", bufs=1))
+
+        slots = keep.tile([P, J // 16], U16)
+        nc.sync.dma_start(slots[:], offs)
+        w1_raw = keep.tile([P, PACK * R], F32, tag="raw")
+        nc.scalar.dma_start(out=w1_raw[:], in_=w1.rearrange("(p t) r -> p (t r)", t=PACK))
+        firsts = keep.tile([P, M // 16], U16)
+        nc.sync.dma_start(firsts[:], offs2)
+        table_words = keep.tile([P, T], I32, align_bytes=64, tag="words")
+        nc.sync.dma_start(out=table_words[:], in_=tab_words[0].rearrange("p c t -> p (c t)").bitcast(I32))
+        seconds = keep.tile([P, M // 16], U16)
+        nc.sync.dma_start(seconds[:], offs3)
+        table_scales = keep.tile([P, T], U8, align_bytes=64)
+        nc.vector.memset(table_scales[:].bitcast(I32), 0)
+        for q in range(4):
+            nc.scalar.dma_start(
+                out=table_scales[32 * q : 32 * q + 4, :].bitcast(I32),
+                in_=tab_scales[0, 4 * q : 4 * q + 4, :].bitcast(I32),
+            )
+
+        def interleaved(raw):
+            return raw.rearrange("p (t c i) -> p c t i", t=PACK, i=4)
+
+        def grouped_view(g):
+            return g[:].rearrange("p (c i) t -> p c t i", i=4)
+
+        def quantize(grouped, width, name):
+            codes = keep.tile([P, width], U32, align_bytes=64, name=name + "_codes")
+            scales = keep.tile([P, width], U8, align_bytes=64, name=name + "_scales")
+            nc.vector.quantize_mx(out=codes[:].bitcast(FP8X4), scales=scales[:], in_=grouped[:].rearrange("p c t -> p (c t)"))
+            return codes, scales
+
+        w1_grouped = keep.tile([P, R, PACK], BF16, align_bytes=64)
+        nc.vector.tensor_copy(out=grouped_view(w1_grouped), in_=interleaved(w1_raw[:]))
+        w1_codes, w1_scales = quantize(w1_grouped, R, "w1")
+
+        late = keep.tile([P, PACK * R + PACK * M + J + 8], F32, tag="raw")
+        wo_raw = late[:, 0 : PACK * R]
+        dy_raw = late[:, PACK * R : PACK * (R + M)]
+        old_sb = late[:, PACK * (R + M) : PACK * (R + M) + J]
+        reserve_col = late[:, PACK * (R + M) + J : PACK * (R + M) + J + 1]
+        nc.sync.dma_start(out=dy_raw, in_=dy.rearrange("(p t) m -> p (t m)", t=PACK))
+        nc.sync.dma_start(out=wo_raw, in_=wo.rearrange("(p t) r -> p (t r)", t=PACK))
+        nc.sync.dma_start(out=reserve_col, in_=reserve)
+        nc.sync.dma_start(out=old_sb, in_=old)
+
+        placed2 = keep.tile([P, J], F32)
+        placed3 = keep.tile([P, J], F32)
+        nc.vector.memset(placed2[:], 0.0)
+        nc.vector.memset(placed3[:], 0.0)
+
+        picked_scales = keep.tile([P, J], U8, align_bytes=64)
+        nc.vector.tensor_copy(picked_scales[:], table_scales[:].indirect(slots[:]))
+
+        wo_grouped = keep.tile([P, R, PACK], BF16, align_bytes=64)
+
+        h = keep.tile([P, J], F32)
+        for u in range(2):
+            cols = slice(u * HALF, (u + 1) * HALF)
+            picked_words = keep.tile([P, HALF], U32, align_bytes=64, name="picked_words%d" % u)
+            nc.vector.tensor_copy(
+                picked_words[:], table_words[:].bitcast(U32).indirect(slots[:, u * HALF // 16 : (u + 1) * HALF // 16])
+            )
+            sums = psum.tile([P, HALF], F32, name="sums%d" % u)
+            nc.tensor.matmul_mx(
+                out=sums[:], lhsT=w1_codes[:].bitcast(FP8X4), lhsT_scale=w1_scales[:],
+                rhs=picked_words[:].bitcast(FP8X4), rhs_scale=picked_scales[:, cols], start=True, stop=True,
+            )
+            nc.scalar.activation(h[:, cols], sums[:], ACT.Exp)
+
+        dy_grouped = keep.tile([P, M, PACK], BF16, align_bytes=64, tag="words")
+        nc.vector.tensor_copy(out=grouped_view(dy_grouped), in_=interleaved(dy_raw))
+
+        dy_codes, dy_scales = quantize(dy_grouped, M, "dy")
+        parts = [slice(0, M // 2), slice(M // 2, M)]
+        lists = [slice(0, M // 32), slice(M // 32, M // 16)]
+
+        def halves(name):
+            return [keep.tile([P, M // 2], F32, name=name + str(u)) for u in range(2)]
+
+        first, second, pair_sum, inv_root, inv, g, t, v = [
+            halves(n) for n in ("first", "second", "pair_sum", "inv_root", "inv", "g", "t", "v")
+        ]
+        nc.vector.tensor_copy(first[0][:], h[:].indirect(firsts[:, lists[0]]))
+        nc.vector.tensor_copy(second[0][:], h[:].indirect(seconds[:, lists[0]]))
+        nc.vector.tensor_copy(out=grouped_view(wo_grouped), in_=interleaved(wo_raw))
+        nc.vector.tensor_copy(first[1][:], h[:].indirect(firsts[:, lists[1]]))
+        wo_codes, wo_scales = quantize(wo_grouped, R, "wo")
+        c0 = psum.tile([P, M], F32)
+        nc.tensor.matmul_mx(
+            out=c0[:], lhsT=wo_codes[:].bitcast(FP8X4), lhsT_scale=wo_scales[:],
+            rhs=dy_codes[:].bitcast(FP8X4), rhs_scale=dy_scales[:], start=True, stop=True,
+        )
+        nc.vector.tensor_tensor(pair_sum[0][:], first[0][:], second[0][:], ALU.add)
+        nc.vector.tensor_copy(second[1][:], h[:].indirect(seconds[:, lists[1]]))
+        nc.vector.tensor_tensor(pair_sum[1][:], first[1][:], second[1][:], ALU.add)
+        nc.vector.tensor_tensor(g[0][:], c0[:, parts[0]], first[0][:], ALU.mult)
+        nc.vector.tensor_tensor(g[1][:], c0[:, parts[1]], first[1][:], ALU.mult)
+        for u in range(2):
+            nc.scalar.activation(inv_root[u][:], pair_sum[u][:], ACT.Abs_reciprocal_sqrt, bias=reserve_col)
+        for u in range(2):
+            nc.scalar.activation(inv[u][:], inv_root[u][:], ACT.Square)
+        rest = [keep.tile([P, M // 2], F32, name="rest%d" % u, tag="inv_root%d" % u) for u in range(2)]
+        for u in range(2):
+            nc.scalar.activation(rest[u][:], second[u][:], ACT.Identity, bias=reserve_col)
+        for u in range(2):
+            nc.vector.tensor_tensor(t[u][:], g[u][:], inv[u][:], ALU.mult)
+        for u in range(2):
+            nc.vector.tensor_tensor(v[u][:], t[u][:], inv[u][:], ALU.mult)
+        for u in range(2):
+            nc.vector.tensor_tensor(placed3[:].indirect(seconds[:, lists[u]]), v[u][:], second[u][:], ALU.mult)
+            nc.vector.tensor_tensor(placed2[:].indirect(firsts[:, lists[u]]), v[u][:], rest[u][:], ALU.mult)
+        partial = [keep.tile([P, HALF], F32, name="partial%d" % u) for u in range(2)]
+        result = [keep.tile([P, HALF], F32, name="result%d" % u) for u in range(2)]
+        for u in range(2):
+            cols = slice(u * HALF, (u + 1) * HALF)
+            nc.vector.tensor_tensor(partial[u][:], old_sb[:, cols], placed3[:, cols], ALU.subtract)
+        for u in range(2):
+            cols = slice(u * HALF, (u + 1) * HALF)
+            nc.vector.tensor_tensor(result[u][:], partial[u][:], placed2[:, cols], ALU.add)
+            (nc.sync, nc.scalar)[u].dma_start(out=out[:, cols], in_=result[u][:])

@@ -28,20 +28,21 @@ def tile_attend_cratiopairs_kernel(tc, tab_words, tab_scales, w1, reserve, wo, d
         slots = keep.tile([P, J // 16], U16)
         nc.sync.dma_start(slots[:], offs)
         w1_raw = keep.tile([P, PACK * R], F32, tag="raw")
-        nc.scalar.dma_start(out=w1_raw[:], in_=w1.rearrange("(p t) r -> p (t r)", t=PACK))
+        nc.sync.dma_start(out=w1_raw[:], in_=w1.rearrange("(p t) r -> p (t r)", t=PACK))
         firsts = keep.tile([P, M // 16], U16)
         nc.sync.dma_start(firsts[:], offs2)
+        table_scales = keep.tile([P, T], U8, align_bytes=64)
+        nc.vector.memset(table_scales[:, 0 : T // 2].bitcast(I32), 0)
+        nc.gpsimd.memset(table_scales[:, T // 2 : T].bitcast(I32), 0)
+        for q in range(4):
+            (nc.sync, nc.scalar)[q % 2].dma_start(
+                out=table_scales[32 * q : 32 * q + 4, :].bitcast(I32),
+                in_=tab_scales[0, 4 * q : 4 * q + 4, :].bitcast(I32),
+            )
         table_words = keep.tile([P, T], I32, align_bytes=64, tag="words")
         nc.sync.dma_start(out=table_words[:], in_=tab_words[0].rearrange("p c t -> p (c t)").bitcast(I32))
         seconds = keep.tile([P, M // 16], U16)
         nc.sync.dma_start(seconds[:], offs3)
-        table_scales = keep.tile([P, T], U8, align_bytes=64)
-        nc.vector.memset(table_scales[:].bitcast(I32), 0)
-        for q in range(4):
-            nc.scalar.dma_start(
-                out=table_scales[32 * q : 32 * q + 4, :].bitcast(I32),
-                in_=tab_scales[0, 4 * q : 4 * q + 4, :].bitcast(I32),
-            )
 
         def interleaved(raw):
             return raw.rearrange("p (t c i) -> p c t i", t=PACK, i=4)

from contextlib import ExitStack

import concourse.mybir as mybir

K, R, F, T, J, M = 512, 128, 512, 2048, 512, 256
FLOPS = 2 * K * R * J + 2 * F * R * M

F32 = mybir.dt.float32
BF16 = mybir.dt.bfloat16
I32 = mybir.dt.int32
U32 = mybir.dt.uint32
U16 = mybir.dt.uint16
U8 = mybir.dt.uint8
FP8X4 = mybir.dt.float8_e4m3fn_x4
ACT = mybir.ActivationFunctionType
ALU = mybir.AluOpType
P = 128
PACK = 4
HALF = J // 2


def tile_attend_cratiopairs_kernel(tc, tab_words, tab_scales, w1, reserve, wo, dy, old, offs, offs2, offs3, out):
    nc = tc.nc
    with ExitStack() as ctx:
        keep = ctx.enter_context(tc.tile_pool(name="keep", bufs=1))
        psum = ctx.enter_context(tc.psum_pool(name="psum", bufs=1))

        slots = keep.tile([P, J // 16], U16)
        nc.sync.dma_start(slots[:], offs)
        w1_raw = keep.tile([P, PACK * R], F32, tag="raw")
        nc.sync.dma_start(out=w1_raw[:], in_=w1.rearrange("(p t) r -> p (t r)", t=PACK))
        firsts = keep.tile([P, M // 16], U16)
        nc.sync.dma_start(firsts[:], offs2)
        table_scales = keep.tile([P, T], U8, align_bytes=64)
        nc.vector.memset(table_scales[:, 0 : T // 2].bitcast(I32), 0)
        nc.gpsimd.memset(table_scales[:, T // 2 : T].bitcast(I32), 0)
        for q in range(4):
            (nc.sync, nc.scalar)[q % 2].dma_start(
                out=table_scales[32 * q : 32 * q + 4, :].bitcast(I32),
                in_=tab_scales[0, 4 * q : 4 * q + 4, :].bitcast(I32),
            )
        table_words = keep.tile([P, T], I32, align_bytes=64, tag="words")
        nc.sync.dma_start(out=table_words[:], in_=tab_words[0].rearrange("p c t -> p (c t)").bitcast(I32))
        seconds = keep.tile([P, M // 16], U16)
        nc.sync.dma_start(seconds[:], offs3)

        def interleaved(raw):
            return raw.rearrange("p (t c i) -> p c t i", t=PACK, i=4)

        def grouped_view(g):
            return g[:].rearrange("p (c i) t -> p c t i", i=4)

        def quantize(grouped, width, name):
            codes = keep.tile([P, width], U32, align_bytes=64, name=name + "_codes")
            scales = keep.tile([P, width], U8, align_bytes=64, name=name + "_scales")
            nc.vector.quantize_mx(out=codes[:].bitcast(FP8X4), scales=scales[:], in_=grouped[:].rearrange("p c t -> p (c t)"))
            return codes, scales

        w1_grouped = keep.tile([P, R, PACK], BF16, align_bytes=64)
        nc.vector.tensor_copy(out=grouped_view(w1_grouped), in_=interleaved(w1_raw[:]))
        w1_codes, w1_scales = quantize(w1_grouped, R, "w1")

        late = keep.tile([P, PACK * R + PACK * M + J + 8], F32, tag="raw")
        wo_raw = late[:, 0 : PACK * R]
        dy_raw = late[:, PACK * R : PACK * (R + M)]
        old_sb = late[:, PACK * (R + M) : PACK * (R + M) + J]
        reserve_col = late[:, PACK * (R + M) + J : PACK * (R + M) + J + 1]
        nc.sync.dma_start(out=dy_raw, in_=dy.rearrange("(p t) m -> p (t m)", t=PACK))
        nc.sync.dma_start(out=wo_raw, in_=wo.rearrange("(p t) r -> p (t r)", t=PACK))
        nc.sync.dma_start(out=reserve_col, in_=reserve)
        nc.sync.dma_start(out=old_sb, in_=old)

        placed2 = keep.tile([P, J], F32)
        placed3 = keep.tile([P, J], F32)
        nc.vector.memset(placed2[:], 0.0)
        nc.vector.memset(placed3[:], 0.0)

        picked_scales = keep.tile([P, J], U8, align_bytes=64)
        nc.vector.tensor_copy(picked_scales[:], table_scales[:].indirect(slots[:]))

        wo_grouped = keep.tile([P, R, PACK], BF16, align_bytes=64)

        h = keep.tile([P, J], F32)
        for u in range(2):
            cols = slice(u * HALF, (u + 1) * HALF)
            picked_words = keep.tile([P, HALF], U32, align_bytes=64, name="picked_words%d" % u)
            nc.vector.tensor_copy(
                picked_words[:], table_words[:].bitcast(U32).indirect(slots[:, u * HALF // 16 : (u + 1) * HALF // 16])
            )
            sums = psum.tile([P, HALF], F32, name="sums%d" % u)
            nc.tensor.matmul_mx(
                out=sums[:], lhsT=w1_codes[:].bitcast(FP8X4), lhsT_scale=w1_scales[:],
                rhs=picked_words[:].bitcast(FP8X4), rhs_scale=picked_scales[:, cols], start=True, stop=True,
            )
            nc.scalar.activation(h[:, cols], sums[:], ACT.Exp)

        dy_grouped = keep.tile([P, M, PACK], BF16, align_bytes=64, tag="words")
        nc.vector.tensor_copy(out=grouped_view(dy_grouped), in_=interleaved(dy_raw))

        dy_codes, dy_scales = quantize(dy_grouped, M, "dy")
        parts = [slice(0, M // 2), slice(M // 2, M)]
        lists = [slice(0, M // 32), slice(M // 32, M // 16)]

        def halves(name):
            return [keep.tile([P, M // 2], F32, name=name + str(u)) for u in range(2)]

        first, second, pair_sum, inv_root, inv, g, t, v = [
            halves(n) for n in ("first", "second", "pair_sum", "inv_root", "inv", "g", "t", "v")
        ]
        nc.vector.tensor_copy(first[0][:], h[:].indirect(firsts[:, lists[0]]))
        nc.vector.tensor_copy(second[0][:], h[:].indirect(seconds[:, lists[0]]))
        nc.vector.tensor_copy(out=grouped_view(wo_grouped), in_=interleaved(wo_raw))
        nc.vector.tensor_copy(first[1][:], h[:].indirect(firsts[:, lists[1]]))
        wo_codes, wo_scales = quantize(wo_grouped, R, "wo")
        c0 = psum.tile([P, M], F32)
        nc.tensor.matmul_mx(
            out=c0[:], lhsT=wo_codes[:].bitcast(FP8X4), lhsT_scale=wo_scales[:],
            rhs=dy_codes[:].bitcast(FP8X4), rhs_scale=dy_scales[:], start=True, stop=True,
        )
        nc.vector.tensor_tensor(pair_sum[0][:], first[0][:], second[0][:], ALU.add)
        nc.vector.tensor_copy(second[1][:], h[:].indirect(seconds[:, lists[1]]))
        nc.vector.tensor_tensor(pair_sum[1][:], first[1][:], second[1][:], ALU.add)
        nc.vector.tensor_tensor(g[0][:], c0[:, parts[0]], first[0][:], ALU.mult)
        nc.vector.tensor_tensor(g[1][:], c0[:, parts[1]], first[1][:], ALU.mult)
        for u in range(2):
            nc.scalar.activation(inv_root[u][:], pair_sum[u][:], ACT.Abs_reciprocal_sqrt, bias=reserve_col)
        for u in range(2):
            nc.scalar.activation(inv[u][:], inv_root[u][:], ACT.Square)
        rest = [keep.tile([P, M // 2], F32, name="rest%d" % u, tag="inv_root%d" % u) for u in range(2)]
        for u in range(2):
            nc.scalar.activation(rest[u][:], second[u][:], ACT.Identity, bias=reserve_col)
        for u in range(2):
            nc.vector.tensor_tensor(t[u][:], g[u][:], inv[u][:], ALU.mult)
        for u in range(2):
            nc.vector.tensor_tensor(v[u][:], t[u][:], inv[u][:], ALU.mult)
        for u in range(2):
            nc.vector.tensor_tensor(placed3[:].indirect(seconds[:, lists[u]]), v[u][:], second[u][:], ALU.mult)
            nc.vector.tensor_tensor(placed2[:].indirect(firsts[:, lists[u]]), v[u][:], rest[u][:], ALU.mult)
        partial = [keep.tile([P, HALF], F32, name="partial%d" % u) for u in range(2)]
        result = [keep.tile([P, HALF], F32, name="result%d" % u) for u in range(2)]
        for u in range(2):
            cols = slice(u * HALF, (u + 1) * HALF)
            nc.vector.tensor_tensor(partial[u][:], old_sb[:, cols], placed3[:, cols], ALU.subtract)
        for u in range(2):
            cols = slice(u * HALF, (u + 1) * HALF)
            nc.vector.tensor_tensor(result[u][:], partial[u][:], placed2[:, cols], ALU.add)
            (nc.sync, nc.scalar)[u].dma_start(out=out[:, cols], in_=result[u][:])
